import numpy as np
import ml_dtypes


def mxq(x, axis, fmt="e4m3"):
    dtype, down = {"e4m3": (ml_dtypes.float8_e4m3fn, 7), "e5m2": (ml_dtypes.float8_e5m2, 14)}[fmt]
    v = np.moveaxis(np.asarray(x, np.float32).astype(ml_dtypes.bfloat16).astype(np.float64), axis, -1)
    blocks = v.reshape(v.shape[:-1] + (-1, 32))
    amax = np.abs(blocks).max(-1, keepdims=True)
    byte = np.maximum(np.where(amax > 0, np.frexp(amax)[1] - 1 + 127, 0) - down, 1)
    scale = np.exp2(byte - 127.0)
    codes = (blocks / scale).astype(np.float32).astype(dtype).astype(np.float64)
    return np.moveaxis((codes * scale).reshape(v.shape), -1, axis)


WIDE = False


def mx_kscale(k):
    if not WIDE:
        return np.ones(k)
    levels = np.array([10, -10, 5, -5, 0])
    if k % 512:
        return np.exp2(np.random.permutation(np.resize(levels, k // 32))).repeat(32)
    a = np.empty((k // 512, 16))
    for p in range(k // 512):
        a[p, :8] = np.random.permutation(np.resize(levels, 8))
        for g in range(8):
            far = levels[np.abs(levels - a[p, g]) >= 10]
            a[p, g + 8] = far[np.random.randint(len(far))]
    return np.exp2(a.ravel()).repeat(32)


def f64(x):
    return np.asarray(x).astype(np.float64)


def striped(idx):
    return np.tile(np.asarray(idx).reshape(-1, 16).T, (8, 1)).astype(np.uint16)


def unstriped(offs):
    return offs[:16].T.reshape(-1).astype(np.int64)


E2M1 = np.array([0.0, 0.5, 1.0, 1.5, 2.0, 3.0, 4.0, 6.0, -0.0, -0.5, -1.0, -1.5, -2.0, -3.0, -4.0, -6.0])


def pack_weight(w, fmt):
    k, n = w.shape
    w = f64(np.asarray(w, np.float32).astype(ml_dtypes.bfloat16)).reshape(k // 32, 32, n)
    amax = np.abs(w).max(1)
    if fmt == "e4m3":
        byte = np.frexp(amax)[1] - 1 + 127 - 7
    else:
        mant, ex = np.frexp(amax / 6.0)
        byte = np.where(mant > 0.5, ex, ex - 1) + 127
    byte = np.clip(np.where(amax > 0, byte, 1), 1, 254)
    scaled = (w * np.exp2(127.0 - byte)[:, None, :]).reshape(k, n).astype(np.float32)
    by_word = np.ascontiguousarray(scaled.reshape(k // 512, 128, 4, n).transpose(0, 1, 3, 2))
    if fmt == "e4m3":
        words = by_word.astype(ml_dtypes.float8_e4m3fn).view(np.uint8)
    else:
        c = by_word.astype(ml_dtypes.float4_e2m1fn).view(np.uint8) & 0xF
        words = (c[..., 0::2] | (c[..., 1::2] << 4)).reshape(k // 512, 128, 2 * n)
    return np.ascontiguousarray(words), np.ascontiguousarray(byte.astype(np.uint8).reshape(k // 512, 16, n))


def unpack_weight(words, scales, fmt):
    g, _, n = scales.shape
    words = np.ascontiguousarray(words).reshape(g, 128, n, -1)
    if fmt == "e4m3":
        vals = words.view(ml_dtypes.float8_e4m3fn).astype(np.float64)
    else:
        nib = np.empty((g, 128, n, 4), np.uint8)
        nib[..., 0::2] = words & 0xF
        nib[..., 1::2] = words >> 4
        vals = E2M1[nib]
    vals = vals * np.repeat(np.exp2(scales.astype(np.float64) - 127.0), 8, axis=1)[..., None]
    return vals.transpose(0, 1, 3, 2).reshape(g * 512, n)


def bf(x):
    return np.asarray(x, np.float32).astype(ml_dtypes.bfloat16)


def planes(Y):
    r, m = Y.shape
    b = f64(bf(Y)).reshape(r // 32, 32, m)
    amax = np.abs(b).max(1)
    byte = np.clip(np.where(amax > 0, np.frexp(amax)[1] - 1 + 127 - 7, 1), 1, 254)
    codes = (b * np.exp2(127.0 - byte)[:, None, :]).reshape(r, m).astype(np.float32).astype(ml_dtypes.float8_e4m3fn).view(np.uint8)
    words = codes.reshape(r // 512, 128, 4, m).transpose(0, 1, 3, 2)
    return np.ascontiguousarray(words), np.ascontiguousarray(byte.astype(np.uint8).reshape(r // 512, 16, m))


K, T, I, J, L, N = 512, 1024, 512, 256, 512, 512


def setup_inputs():
    n = np.random.standard_normal
    idx = np.random.permutation(T)[:I]
    idx2 = np.random.randint(0, I, J)
    fk = mx_kscale(K)
    fl = mx_kscale(L)
    xtp = pack_weight(n((K, T)) / fk[:, None], "e4m3")
    wp = pack_weight(n((K, N)) * 1 / np.sqrt(K) * fk[:, None], "e2m1")
    rqp = pack_weight(n((L, J)) / fl[:, None], "e2m1")
    return {
        "xt_words": xtp[0],
        "xt_scales": xtp[1],
        "w_words": wp[0],
        "w_scales": wp[1],
        "rq_words": rqp[0],
        "rq_scales": rqp[1],
        "wr": (n((L, N)) * 1 / np.sqrt(L) * fl[:, None]).astype(np.float32),
        "di": (np.random.uniform(0.5, 2.0, (1, I))).astype(np.float32),
        "offs": striped(idx),
        "offs2": striped(idx2),
    }


def reference(xt_words, xt_scales, w_words, w_scales, rq_words, rq_scales, wr, di, offs, offs2):
    idx = unstriped(offs)
    idx2 = unstriped(offs2)
    xtu = unpack_weight(xt_words, xt_scales, "e4m3")
    wu = unpack_weight(w_words, w_scales, "e2m1")
    rqu = unpack_weight(rq_words, rq_scales, "e2m1")
    z = wu.T @ xtu
    dz = z[:, idx] * f64(di)
    wrq = mxq(f64(wr), 0, "e4m3")
    r = wrq.T @ rqu
    y = np.tanh(dz[:, idx2]) + r
    words, scales = planes(y)
    return y, words, scales

@@ -1,0 +1,180 @@
+from contextlib import ExitStack
+
+import concourse.mybir as mybir
+from concourse.masks import make_identity
+
+K, T, I, J, L, N = 512, 1024, 512, 256, 512, 512
+FLOPS = 2 * K * N * T + 2 * L * N * J
+
+F32 = mybir.dt.float32
+BF16 = mybir.dt.bfloat16
+I32 = mybir.dt.int32
+U32 = mybir.dt.uint32
+U16 = mybir.dt.uint16
+U8 = mybir.dt.uint8
+FP8X4 = mybir.dt.float8_e4m3fn_x4
+FP4X4 = mybir.dt.float4_e2m1fn_x4
+ACT = mybir.ActivationFunctionType
+ALU = mybir.AluOpType
+
+P = 128
+PACK = 4
+BANK = 512
+
+
+def load_scales(queues, plane, rows):
+    for q in range(4):
+        queues[q].dma_start(out=plane[32 * q : 32 * q + 4, :].bitcast(I32), in_=rows[4 * q : 4 * q + 4, :].bitcast(I32))
+
+
+def tile_list_link_of_link_pl_kernel(tc, xt_words, xt_scales, w_words, w_scales, rq_words, rq_scales, wr, di, offs, offs2, out_0, out_1, out_2):
+    nc = tc.nc
+    with ExitStack() as ctx:
+        sb = ctx.enter_context(tc.tile_pool(name="sb", bufs=1))
+        ps = ctx.enter_context(tc.psum_pool(name="ps", bufs=1))
+        zps = ctx.enter_context(tc.psum_pool(name="zps", bufs=5))
+
+        w_sc_raw = sb.tile([P, N], U8, name="w_sc_raw", align_bytes=64)
+        xt_sc = sb.tile([P, T], U8, name="xt_sc", align_bytes=64)
+        nc.gpsimd.memset(w_sc_raw[:].bitcast(U32), 0)
+        nc.vector.memset(xt_sc[:].bitcast(U32), 0)
+
+        w_raw = sb.tile([P, 2 * N], U8, name="w_raw", tag="w_then_wr", align_bytes=64)
+        nc.sync.dma_start(out=w_raw[:].bitcast(I32), in_=w_words[0].bitcast(I32))
+        list1 = sb.tile([P, I // 16], U16, name="list1")
+        nc.sync.dma_start(list1[:], offs)
+        list2 = sb.tile([P, J // 16], U16, name="list2")
+        nc.sync.dma_start(list2[:], offs2)
+        load_scales([nc.scalar] * 4, w_sc_raw, w_scales[0])
+        xt_view = xt_words[0].rearrange("p c r -> p (c r)").bitcast(I32)
+        xt = sb.tile([P, T], U32, name="xt", align_bytes=64)
+        nc.sync.dma_start(out=xt[:].bitcast(I32), in_=xt_view)
+        di_col = sb.tile([P, PACK], F32, name="di_col", tag="di_then_rq", align_bytes=64)
+        nc.gpsimd.dma_start(out=di_col[:], in_=di[0].rearrange("(p c) -> p c", c=PACK))
+        load_scales([nc.sync, nc.sync, nc.sync, nc.gpsimd], xt_sc, xt_scales[0])
+
+        ident = sb.tile([P, P], F32, name="ident")
+        nc.vector.memset(ident[:], 0.0)
+        make_identity(nc, ident[:], nomemset=True)
+
+        warm = sb.tile([P, 8], F32, name="warm")
+        nc.vector.memset(warm[:, 0:1], 0.0)
+        warm2 = sb.tile([P, 8], F32, name="warm2")
+        nc.scalar.activation(warm2[:, 0:1], warm[:, 0:1], ACT.Sigmoid)
+
+        w_deal = sb.tile([P, 2 * N], U8, name="w_deal", align_bytes=64)
+        nc.vector.tensor_copy(out=w_deal[:].bitcast(U16).rearrange("p (t m) -> p m t", t=PACK), in_=w_raw[:].bitcast(U16).rearrange("p (m t) -> p m t", t=PACK))
+        w_sc = sb.tile([P, N], U8, name="w_sc", align_bytes=64)
+        nc.vector.tensor_copy(out=w_sc[:].rearrange("p (t m) -> p m t", t=PACK), in_=w_sc_raw[:].rearrange("p (m t) -> p m t", t=PACK))
+
+        di_ps = ps.tile([P, PACK, P], F32, name="di_ps")
+        for c in range(PACK):
+            nc.tensor.transpose(di_ps[:, c, :], di_col[:, c : c + 1].to_broadcast([P, P]), ident[:])
+        di_all = sb.tile([P, I], F32, name="di_all")
+        nc.scalar.copy(out=di_all[:].rearrange("p (k c) -> p k c", c=PACK), in_=di_ps[:].rearrange("p c k -> p k c"))
+
+        wr_view = wr.rearrange("(p j) n -> p j n", j=PACK)
+        wr_both = sb.tile([P, 2 * PACK * N // 2], F32, name="wr_both", tag="w_then_wr", align_bytes=64)
+        wr_raw = [wr_both[:, h * PACK * N // 2 : (h + 1) * PACK * N // 2].rearrange("p (j n) -> p j n", j=PACK) for h in range(2)]
+        for h in range(2):
+            nc.sync.dma_start(out=wr_raw[h], in_=wr_view[:, :, h * N // 2 : (h + 1) * N // 2])
+        rq_sc = w_sc_raw[:, 0:J]
+        load_scales([nc.sync] * 4, rq_sc, rq_scales[0])
+        rq = sb.tile([P, 2 * J], U8, name="rq", tag="di_then_rq", align_bytes=64)
+        nc.sync.dma_start(out=rq[:].bitcast(I32), in_=rq_words[0].bitcast(I32))
+
+        z = [sb.tile([P, T], F32, name="z%d" % t) for t in range(PACK)]
+        dz = [sb.tile([P, I], F32, name="dz%d" % t) for t in range(PACK)]
+        sg = [sb.tile([P, J], F32, name="sg%d" % t) for t in range(PACK)]
+        y = sb.tile([P, PACK, J], F32, name="y")
+        out_view = out_0.rearrange("(p t) j -> p t j", t=PACK)
+
+        def z_slice(t):
+            for h in range(2):
+                acc = zps.tile([P, BANK], F32, name="acc")
+                cols = slice(h * BANK, (h + 1) * BANK)
+                nc.tensor.matmul_mx(
+                    out=acc[:],
+                    lhsT=w_deal[:, 2 * P * t : 2 * P * (t + 1)].bitcast(FP4X4),
+                    lhsT_scale=w_sc[:, P * t : P * (t + 1)],
+                    rhs=xt[:, cols].bitcast(FP8X4),
+                    rhs_scale=xt_sc[:, cols],
+                    start=True,
+                    stop=True,
+                )
+                if t == 0 and h == 1:
+                    nc.vector.tensor_copy(out=z[t][:, cols], in_=acc[:])
+                else:
+                    nc.scalar.copy(out=z[t][:, cols], in_=acc[:])
+
+        def look1(t):
+            nc.vector.tensor_tensor(dz[t][:], z[t][:].indirect(list1[:]), di_all[:], ALU.mult)
+
+        def look2(t):
+            nc.scalar.activation(sg[t][:], dz[t][:].indirect(list2[:]), ACT.Sigmoid, scale=2.0)
+
+        wr_bf = sb.tile([P, PACK * P * PACK], BF16, name="wr_bf", align_bytes=64)
+        wr_dst = wr_bf[:].rearrange("p (t m j) -> p m j t", t=PACK, j=PACK)
+
+        def wr_round(h):
+            dst = wr_dst[:, h * P // 2 : (h + 1) * P // 2]
+            src = wr_raw[h].rearrange("p j (m t) -> p m j t", t=PACK)
+            if h == 0:
+                nc.scalar.copy(out=dst, in_=src)
+            else:
+                nc.vector.tensor_copy(out=dst, in_=src)
+
+        wr_codes = sb.tile([P, N], U32, name="wr_codes", align_bytes=64)
+        wr_sc = sb.tile([P, N], U8, name="wr_sc", align_bytes=64)
+        r_less = sb.tile([P, PACK, J], F32, name="r_less")
+
+        def r_all():
+            nc.vector.quantize_mx(out=wr_codes[:].bitcast(FP8X4), scales=wr_sc[:], in_=wr_bf[:])
+            for u in range(2):
+                r_ps = ps.tile([P, 2, J], F32, name="r_ps%d" % u)
+                for e in range(2):
+                    t = 2 * u + e
+                    nc.tensor.matmul_mx(
+                        out=r_ps[:, e, :],
+                        lhsT=wr_codes[:, P * t : P * (t + 1)].bitcast(FP8X4),
+                        lhsT_scale=wr_sc[:, P * t : P * (t + 1)],
+                        rhs=rq[:].bitcast(FP4X4),
+                        rhs_scale=rq_sc,
+                        start=True,
+                        stop=True,
+                    )
+                nc.scalar.activation(r_less[:, 2 * u : 2 * u + 2, :], r_ps[:], ACT.Copy, bias=-1.0)
+
+        def finish(t):
+            nc.vector.scalar_tensor_tensor(y[:, t, :], sg[t][:], 2.0, r_less[:, t, :], ALU.mult, ALU.add)
+            nc.sync.dma_start(out=out_view[:, t, :], in_=y[:, t, :])
+
+        z_slice(0)
+        z_slice(1)
+        look1(0)
+        z_slice(2)
+        look1(1)
+        wr_round(0)
+        z_slice(3)
+        wr_round(1)
+        look1(2)
+        look2(0)
+        look2(1)
+        look2(2)
+        r_all()
+        look1(3)
+        look2(3)
+        finish(0)
+        finish(1)
+        finish(2)
+        finish(3)
+
+        y_bf = sb.tile([P, J * PACK], BF16, name="y_bf", align_bytes=64)
+        nc.vector.tensor_copy(out=y_bf[:].rearrange("p (c i t) -> p c t i", i=4, t=PACK), in_=y[:].rearrange("p t (c i) -> p c t i", i=4))
+        y_codes = sb.tile([P, J], U32, name="y_codes", align_bytes=64)
+        y_sc = sb.tile([P, J], U8, name="y_sc", align_bytes=64)
+        nc.vector.quantize_mx(out=y_codes[:].bitcast(FP8X4), scales=y_sc[:], in_=y_bf[:])
+        nc.sync.dma_start(out=out_1[0].rearrange("p c r -> p (c r)").bitcast(I32), in_=y_codes[:].bitcast(I32))
+        for q in range(4):
+            eng = nc.scalar if q % 2 == 0 else nc.sync
+            eng.dma_start(out=out_2[0][4 * q : 4 * q + 4, :].bitcast(I32), in_=y_sc[32 * q : 32 * q + 4, :].bitcast(I32))

@@ -1,7 +1,6 @@
 from contextlib import ExitStack
 
 import concourse.mybir as mybir
-from concourse.masks import make_identity
 
 K, T, I, J, L, N = 512, 1024, 512, 256, 512, 512
 FLOPS = 2 * K * N * T + 2 * L * N * J
@@ -22,40 +21,49 @@ PACK = 4
 BANK = 512
 
 
-def load_scales(queues, plane, rows):
-    for q in range(4):
-        queues[q].dma_start(out=plane[32 * q : 32 * q + 4, :].bitcast(I32), in_=rows[4 * q : 4 * q + 4, :].bitcast(I32))
+def load_scales(queue, plane, rows, quadrants):
+    for q in quadrants:
+        queue.dma_start(out=plane[32 * q : 32 * q + 4, :].bitcast(I32), in_=rows[4 * q : 4 * q + 4, :].bitcast(I32))
 
 
 def tile_list_link_of_link_pl_kernel(tc, xt_words, xt_scales, w_words, w_scales, rq_words, rq_scales, wr, di, offs, offs2, out_0, out_1, out_2):
     nc = tc.nc
     with ExitStack() as ctx:
         sb = ctx.enter_context(tc.tile_pool(name="sb", bufs=1))
+        reuse = ctx.enter_context(tc.tile_pool(name="reuse", bufs=1))
         ps = ctx.enter_context(tc.psum_pool(name="ps", bufs=1))
-        zps = ctx.enter_context(tc.psum_pool(name="zps", bufs=5))
+        zps = ctx.enter_context(tc.psum_pool(name="zps", bufs=6))
 
         w_sc_raw = sb.tile([P, N], U8, name="w_sc_raw", align_bytes=64)
         xt_sc = sb.tile([P, T], U8, name="xt_sc", align_bytes=64)
-        nc.gpsimd.memset(w_sc_raw[:].bitcast(U32), 0)
-        nc.vector.memset(xt_sc[:].bitcast(U32), 0)
+        nc.vector.memset(w_sc_raw[:].bitcast(U32), 0)
 
-        w_raw = sb.tile([P, 2 * N], U8, name="w_raw", tag="w_then_wr", align_bytes=64)
+        load_scales(nc.sync, xt_sc, xt_scales[0], (0, 1))
+        load_scales(nc.gpsimd, xt_sc, xt_scales[0], (2,))
+        w_raw = sb.tile([P, 2 * N], U8, name="w_raw", align_bytes=64)
         nc.sync.dma_start(out=w_raw[:].bitcast(I32), in_=w_words[0].bitcast(I32))
-        list1 = sb.tile([P, I // 16], U16, name="list1")
-        nc.sync.dma_start(list1[:], offs)
-        list2 = sb.tile([P, J // 16], U16, name="list2")
-        nc.sync.dma_start(list2[:], offs2)
-        load_scales([nc.scalar] * 4, w_sc_raw, w_scales[0])
         xt_view = xt_words[0].rearrange("p c r -> p (c r)").bitcast(I32)
         xt = sb.tile([P, T], U32, name="xt", align_bytes=64)
         nc.sync.dma_start(out=xt[:].bitcast(I32), in_=xt_view)
-        di_col = sb.tile([P, PACK], F32, name="di_col", tag="di_then_rq", align_bytes=64)
-        nc.gpsimd.dma_start(out=di_col[:], in_=di[0].rearrange("(p c) -> p c", c=PACK))
-        load_scales([nc.sync, nc.sync, nc.sync, nc.gpsimd], xt_sc, xt_scales[0])
+        load_scales(nc.sync, w_sc_raw, w_scales[0], range(4))
+        load_scales(nc.sync, xt_sc, xt_scales[0], (3,))
 
-        ident = sb.tile([P, P], F32, name="ident")
-        nc.vector.memset(ident[:], 0.0)
-        make_identity(nc, ident[:], nomemset=True)
+        wr_view = wr.rearrange("(p j) n -> p j n", j=PACK)
+        wr_lo = sb.tile([P, PACK, N // 2], F32, name="wr_lo")
+        wr_hi = reuse.tile([P, PACK, N // 2], F32, name="wr_hi", offset=2048)
+        wr_raw = [wr_lo[:], wr_hi[:]]
+        nc.sync.dma_start(out=wr_lo[:], in_=wr_view[:, :, 0 : N // 2])
+        nc.sync.dma_start(out=wr_hi[:], in_=wr_view[:, :, N // 2 : N])
+        list1 = sb.tile([P, I // 16], U16, name="list1")
+        nc.sync.dma_start(list1[:], offs)
+        di_all = sb.tile([P, I], F32, name="di_all")
+        nc.sync.dma_start(out=di_all[:], in_=di[0].partition_broadcast(P))
+        list2 = sb.tile([P, J // 16], U16, name="list2")
+        nc.sync.dma_start(list2[:], offs2)
+        rq_sc = sb.tile([P, J], U8, name="rq_sc", align_bytes=64)
+        load_scales(nc.sync, rq_sc, rq_scales[0], range(4))
+        rq = sb.tile([P, 2 * J], U8, name="rq", align_bytes=64)
+        nc.sync.dma_start(out=rq[:].bitcast(I32), in_=rq_words[0].bitcast(I32))
 
         warm = sb.tile([P, 8], F32, name="warm")
         nc.vector.memset(warm[:, 0:1], 0.0)
@@ -67,25 +75,17 @@ def tile_list_link_of_link_pl_kernel(tc, xt_words, xt_scales, w_words, w_scales,
         w_sc = sb.tile([P, N], U8, name="w_sc", align_bytes=64)
         nc.vector.tensor_copy(out=w_sc[:].rearrange("p (t m) -> p m t", t=PACK), in_=w_sc_raw[:].rearrange("p (m t) -> p m t", t=PACK))
 
-        di_ps = ps.tile([P, PACK, P], F32, name="di_ps")
-        for c in range(PACK):
-            nc.tensor.transpose(di_ps[:, c, :], di_col[:, c : c + 1].to_broadcast([P, P]), ident[:])
-        di_all = sb.tile([P, I], F32, name="di_all")
-        nc.scalar.copy(out=di_all[:].rearrange("p (k c) -> p k c", c=PACK), in_=di_ps[:].rearrange("p c k -> p k c"))
-
-        wr_view = wr.rearrange("(p j) n -> p j n", j=PACK)
-        wr_both = sb.tile([P, 2 * PACK * N // 2], F32, name="wr_both", tag="w_then_wr", align_bytes=64)
-        wr_raw = [wr_both[:, h * PACK * N // 2 : (h + 1) * PACK * N // 2].rearrange("p (j n) -> p j n", j=PACK) for h in range(2)]
-        for h in range(2):
-            nc.sync.dma_start(out=wr_raw[h], in_=wr_view[:, :, h * N // 2 : (h + 1) * N // 2])
-        rq_sc = w_sc_raw[:, 0:J]
-        load_scales([nc.sync] * 4, rq_sc, rq_scales[0])
-        rq = sb.tile([P, 2 * J], U8, name="rq", tag="di_then_rq", align_bytes=64)
-        nc.sync.dma_start(out=rq[:].bitcast(I32), in_=rq_words[0].bitcast(I32))
-
-        z = [sb.tile([P, T], F32, name="z%d" % t) for t in range(PACK)]
-        dz = [sb.tile([P, I], F32, name="dz%d" % t) for t in range(PACK)]
-        sg = [sb.tile([P, J], F32, name="sg%d" % t) for t in range(PACK)]
+        wr_bf = reuse.tile([P, PACK * P * PACK], BF16, name="wr_bf", align_bytes=64, offset=7168)
+        z = [sb.tile([P, T], F32, name="z%d" % t) for t in range(PACK - 1)]
+        z.append(reuse.tile([P, T], F32, name="z3", offset=0))
+        dz = [
+            reuse.tile([P, I], F32, name="dz0", offset=6144),
+            reuse.tile([P, I], F32, name="dz1", offset=8192),
+            reuse.tile([P, I], F32, name="dz2", offset=10240),
+            reuse.tile([P, I], F32, name="dz3", offset=4096),
+        ]
+        y_plus = sb.tile([P, PACK, J], F32, name="y_plus")
+        sg = sb.tile([P, PACK, J], F32, name="sg")
         y = sb.tile([P, PACK, J], F32, name="y")
         out_view = out_0.rearrange("(p t) j -> p t j", t=PACK)
 
@@ -102,7 +102,7 @@ def tile_list_link_of_link_pl_kernel(tc, xt_words, xt_scales, w_words, w_scales,
                     start=True,
                     stop=True,
                 )
-                if t == 0 and h == 1:
+                if t == 3 and h == 1:
                     nc.vector.tensor_copy(out=z[t][:, cols], in_=acc[:])
                 else:
                     nc.scalar.copy(out=z[t][:, cols], in_=acc[:])
@@ -111,66 +111,66 @@ def tile_list_link_of_link_pl_kernel(tc, xt_words, xt_scales, w_words, w_scales,
             nc.vector.tensor_tensor(dz[t][:], z[t][:].indirect(list1[:]), di_all[:], ALU.mult)
 
         def look2(t):
-            nc.scalar.activation(sg[t][:], dz[t][:].indirect(list2[:]), ACT.Sigmoid, scale=2.0)
+            nc.scalar.activation(sg[:, t, :], dz[t][:].indirect(list2[:]), ACT.Sigmoid, scale=2.0)
 
-        wr_bf = sb.tile([P, PACK * P * PACK], BF16, name="wr_bf", align_bytes=64)
         wr_dst = wr_bf[:].rearrange("p (t m j) -> p m j t", t=PACK, j=PACK)
 
         def wr_round(h):
             dst = wr_dst[:, h * P // 2 : (h + 1) * P // 2]
             src = wr_raw[h].rearrange("p j (m t) -> p m j t", t=PACK)
-            if h == 0:
-                nc.scalar.copy(out=dst, in_=src)
-            else:
-                nc.vector.tensor_copy(out=dst, in_=src)
+            nc.vector.tensor_copy(out=dst, in_=src)
 
         wr_codes = sb.tile([P, N], U32, name="wr_codes", align_bytes=64)
         wr_sc = sb.tile([P, N], U8, name="wr_sc", align_bytes=64)
-        r_less = sb.tile([P, PACK, J], F32, name="r_less")
+        r_ps = [ps.tile([P, 2, J], F32, name="r_ps%d" % u) for u in range(2)]
 
         def r_all():
             nc.vector.quantize_mx(out=wr_codes[:].bitcast(FP8X4), scales=wr_sc[:], in_=wr_bf[:])
             for u in range(2):
-                r_ps = ps.tile([P, 2, J], F32, name="r_ps%d" % u)
                 for e in range(2):
                     t = 2 * u + e
                     nc.tensor.matmul_mx(
-                        out=r_ps[:, e, :],
+                        out=r_ps[u][:, e, :],
                         lhsT=wr_codes[:, P * t : P * (t + 1)].bitcast(FP8X4),
                         lhsT_scale=wr_sc[:, P * t : P * (t + 1)],
                         rhs=rq[:].bitcast(FP4X4),
-                        rhs_scale=rq_sc,
+                        rhs_scale=rq_sc[:],
                         start=True,
                         stop=True,
                     )
-                nc.scalar.activation(r_less[:, 2 * u : 2 * u + 2, :], r_ps[:], ACT.Copy, bias=-1.0)
 
-        def finish(t):
-            nc.vector.scalar_tensor_tensor(y[:, t, :], sg[t][:], 2.0, r_less[:, t, :], ALU.mult, ALU.add)
-            nc.sync.dma_start(out=out_view[:, t, :], in_=y[:, t, :])
+        def add_r(t0, t1):
+            nc.vector.scalar_tensor_tensor(y_plus[:, t0:t1, :], sg[:, t0:t1, :], 2.0, r_ps[t0 // 2][:, t0 % 2 : t0 % 2 + t1 - t0, :], ALU.mult, ALU.add)
+
+        def store_y(t0, t1):
+            nc.scalar.activation(y[:, t0:t1, :], y_plus[:, t0:t1, :], ACT.Copy, bias=-1.0)
+            nc.sync.dma_start(out=out_view[:, t0:t1, :], in_=y[:, t0:t1, :])
 
         z_slice(0)
         z_slice(1)
-        look1(0)
         z_slice(2)
-        look1(1)
         wr_round(0)
-        z_slice(3)
         wr_round(1)
-        look1(2)
-        look2(0)
-        look2(1)
-        look2(2)
         r_all()
+        look1(0)
+        look1(1)
+        z_slice(3)
+        look2(0)
+        look1(2)
+        look2(1)
         look1(3)
+        look2(2)
         look2(3)
-        finish(0)
-        finish(1)
-        finish(2)
-        finish(3)
+        add_r(0, 2)
+        add_r(2, 3)
+        add_r(3, 4)
+        store_y(0, 2)
+        store_y(2, 4)
 
         y_bf = sb.tile([P, J * PACK], BF16, name="y_bf", align_bytes=64)
-        nc.vector.tensor_copy(out=y_bf[:].rearrange("p (c i t) -> p c t i", i=4, t=PACK), in_=y[:].rearrange("p t (c i) -> p c t i", i=4))
+        y_dst = y_bf[:].rearrange("p (c i t) -> p c t i", i=4, t=PACK)
+        y_src = y_plus[:].rearrange("p t (c i) -> p c t i", i=4)
+        nc.vector.tensor_scalar(y_dst, y_src, -1.0, None, ALU.add)
         y_codes = sb.tile([P, J], U32, name="y_codes", align_bytes=64)
         y_sc = sb.tile([P, J], U8, name="y_sc", align_bytes=64)
         nc.vector.quantize_mx(out=y_codes[:].bitcast(FP8X4), scales=y_sc[:], in_=y_bf[:])

from contextlib import ExitStack

import concourse.mybir as mybir

K, T, I, J, L, N = 512, 1024, 512, 256, 512, 512
FLOPS = 2 * K * N * T + 2 * L * N * J

F32 = mybir.dt.float32
BF16 = mybir.dt.bfloat16
I32 = mybir.dt.int32
U32 = mybir.dt.uint32
U16 = mybir.dt.uint16
U8 = mybir.dt.uint8
FP8X4 = mybir.dt.float8_e4m3fn_x4
FP4X4 = mybir.dt.float4_e2m1fn_x4
ACT = mybir.ActivationFunctionType
ALU = mybir.AluOpType

P = 128
PACK = 4
BANK = 512


def load_scales(queue, plane, rows, quadrants):
    for q in quadrants:
        queue.dma_start(out=plane[32 * q : 32 * q + 4, :].bitcast(I32), in_=rows[4 * q : 4 * q + 4, :].bitcast(I32))


def tile_list_link_of_link_pl_kernel(tc, xt_words, xt_scales, w_words, w_scales, rq_words, rq_scales, wr, di, offs, offs2, out_0, out_1, out_2):
    nc = tc.nc
    with ExitStack() as ctx:
        sb = ctx.enter_context(tc.tile_pool(name="sb", bufs=1))
        reuse = ctx.enter_context(tc.tile_pool(name="reuse", bufs=1))
        ps = ctx.enter_context(tc.psum_pool(name="ps", bufs=1))
        zps = ctx.enter_context(tc.psum_pool(name="zps", bufs=6))

        w_sc_raw = sb.tile([P, N], U8, name="w_sc_raw", align_bytes=64)
        xt_sc = sb.tile([P, T], U8, name="xt_sc", align_bytes=64)
        nc.vector.memset(w_sc_raw[:].bitcast(U32), 0)

        load_scales(nc.sync, xt_sc, xt_scales[0], (0, 1))
        load_scales(nc.gpsimd, xt_sc, xt_scales[0], (2,))
        w_raw = sb.tile([P, 2 * N], U8, name="w_raw", align_bytes=64)
        nc.sync.dma_start(out=w_raw[:].bitcast(I32), in_=w_words[0].bitcast(I32))
        xt_view = xt_words[0].rearrange("p c r -> p (c r)").bitcast(I32)
        xt = sb.tile([P, T], U32, name="xt", align_bytes=64)
        nc.sync.dma_start(out=xt[:].bitcast(I32), in_=xt_view)
        load_scales(nc.sync, w_sc_raw, w_scales[0], range(4))
        load_scales(nc.sync, xt_sc, xt_scales[0], (3,))

        wr_view = wr.rearrange("(p j) n -> p j n", j=PACK)
        wr_lo = sb.tile([P, PACK, N // 2], F32, name="wr_lo")
        wr_hi = reuse.tile([P, PACK, N // 2], F32, name="wr_hi", offset=2048)
        wr_raw = [wr_lo[:], wr_hi[:]]
        nc.sync.dma_start(out=wr_lo[:], in_=wr_view[:, :, 0 : N // 2])
        nc.sync.dma_start(out=wr_hi[:], in_=wr_view[:, :, N // 2 : N])
        list1 = sb.tile([P, I // 16], U16, name="list1")
        nc.sync.dma_start(list1[:], offs)
        di_all = sb.tile([P, I], F32, name="di_all")
        nc.sync.dma_start(out=di_all[:], in_=di[0].partition_broadcast(P))
        list2 = sb.tile([P, J // 16], U16, name="list2")
        nc.sync.dma_start(list2[:], offs2)
        rq_sc = sb.tile([P, J], U8, name="rq_sc", align_bytes=64)
        load_scales(nc.sync, rq_sc, rq_scales[0], range(4))
        rq = sb.tile([P, 2 * J], U8, name="rq", align_bytes=64)
        nc.sync.dma_start(out=rq[:].bitcast(I32), in_=rq_words[0].bitcast(I32))

        warm = sb.tile([P, 8], F32, name="warm")
        nc.vector.memset(warm[:, 0:1], 0.0)
        warm2 = sb.tile([P, 8], F32, name="warm2")
        nc.scalar.activation(warm2[:, 0:1], warm[:, 0:1], ACT.Sigmoid)

        w_deal = sb.tile([P, 2 * N], U8, name="w_deal", align_bytes=64)
        nc.vector.tensor_copy(out=w_deal[:].bitcast(U16).rearrange("p (t m) -> p m t", t=PACK), in_=w_raw[:].bitcast(U16).rearrange("p (m t) -> p m t", t=PACK))
        w_sc = sb.tile([P, N], U8, name="w_sc", align_bytes=64)
        nc.vector.tensor_copy(out=w_sc[:].rearrange("p (t m) -> p m t", t=PACK), in_=w_sc_raw[:].rearrange("p (m t) -> p m t", t=PACK))

        wr_bf = reuse.tile([P, PACK * P * PACK], BF16, name="wr_bf", align_bytes=64, offset=7168)
        z = [sb.tile([P, T], F32, name="z%d" % t) for t in range(PACK - 1)]
        z.append(reuse.tile([P, T], F32, name="z3", offset=0))
        dz = [
            reuse.tile([P, I], F32, name="dz0", offset=6144),
            reuse.tile([P, I], F32, name="dz1", offset=8192),
            reuse.tile([P, I], F32, name="dz2", offset=10240),
            reuse.tile([P, I], F32, name="dz3", offset=4096),
        ]
        y_plus = sb.tile([P, PACK, J], F32, name="y_plus")
        sg = sb.tile([P, PACK, J], F32, name="sg")
        y = sb.tile([P, PACK, J], F32, name="y")
        out_view = out_0.rearrange("(p t) j -> p t j", t=PACK)

        def z_slice(t):
            for h in range(2):
                acc = zps.tile([P, BANK], F32, name="acc")
                cols = slice(h * BANK, (h + 1) * BANK)
                nc.tensor.matmul_mx(
                    out=acc[:],
                    lhsT=w_deal[:, 2 * P * t : 2 * P * (t + 1)].bitcast(FP4X4),
                    lhsT_scale=w_sc[:, P * t : P * (t + 1)],
                    rhs=xt[:, cols].bitcast(FP8X4),
                    rhs_scale=xt_sc[:, cols],
                    start=True,
                    stop=True,
                )
                if t == 3 and h == 1:
                    nc.vector.tensor_copy(out=z[t][:, cols], in_=acc[:])
                else:
                    nc.scalar.copy(out=z[t][:, cols], in_=acc[:])

        def look1(t):
            nc.vector.tensor_tensor(dz[t][:], z[t][:].indirect(list1[:]), di_all[:], ALU.mult)

        def look2(t):
            nc.scalar.activation(sg[:, t, :], dz[t][:].indirect(list2[:]), ACT.Sigmoid, scale=2.0)

        wr_dst = wr_bf[:].rearrange("p (t m j) -> p m j t", t=PACK, j=PACK)

        def wr_round(h):
            dst = wr_dst[:, h * P // 2 : (h + 1) * P // 2]
            src = wr_raw[h].rearrange("p j (m t) -> p m j t", t=PACK)
            nc.vector.tensor_copy(out=dst, in_=src)

        wr_codes = sb.tile([P, N], U32, name="wr_codes", align_bytes=64)
        wr_sc = sb.tile([P, N], U8, name="wr_sc", align_bytes=64)
        r_ps = [ps.tile([P, 2, J], F32, name="r_ps%d" % u) for u in range(2)]

        def r_all():
            nc.vector.quantize_mx(out=wr_codes[:].bitcast(FP8X4), scales=wr_sc[:], in_=wr_bf[:])
            for u in range(2):
                for e in range(2):
                    t = 2 * u + e
                    nc.tensor.matmul_mx(
                        out=r_ps[u][:, e, :],
                        lhsT=wr_codes[:, P * t : P * (t + 1)].bitcast(FP8X4),
                        lhsT_scale=wr_sc[:, P * t : P * (t + 1)],
                        rhs=rq[:].bitcast(FP4X4),
                        rhs_scale=rq_sc[:],
                        start=True,
                        stop=True,
                    )

        def add_r(t0, t1):
            nc.vector.scalar_tensor_tensor(y_plus[:, t0:t1, :], sg[:, t0:t1, :], 2.0, r_ps[t0 // 2][:, t0 % 2 : t0 % 2 + t1 - t0, :], ALU.mult, ALU.add)

        def store_y(t0, t1):
            nc.scalar.activation(y[:, t0:t1, :], y_plus[:, t0:t1, :], ACT.Copy, bias=-1.0)
            nc.sync.dma_start(out=out_view[:, t0:t1, :], in_=y[:, t0:t1, :])

        z_slice(0)
        z_slice(1)
        z_slice(2)
        wr_round(0)
        wr_round(1)
        r_all()
        look1(0)
        look1(1)
        z_slice(3)
        look2(0)
        look1(2)
        look2(1)
        look1(3)
        look2(2)
        look2(3)
        add_r(0, 2)
        add_r(2, 3)
        add_r(3, 4)
        store_y(0, 2)
        store_y(2, 4)

        y_bf = sb.tile([P, J * PACK], BF16, name="y_bf", align_bytes=64)
        y_dst = y_bf[:].rearrange("p (c i t) -> p c t i", i=4, t=PACK)
        y_src = y_plus[:].rearrange("p t (c i) -> p c t i", i=4)
        nc.vector.tensor_scalar(y_dst, y_src, -1.0, None, ALU.add)
        y_codes = sb.tile([P, J], U32, name="y_codes", align_bytes=64)
        y_sc = sb.tile([P, J], U8, name="y_sc", align_bytes=64)
        nc.vector.quantize_mx(out=y_codes[:].bitcast(FP8X4), scales=y_sc[:], in_=y_bf[:])
        nc.sync.dma_start(out=out_1[0].rearrange("p c r -> p (c r)").bitcast(I32), in_=y_codes[:].bitcast(I32))
        for q in range(4):
            eng = nc.scalar if q % 2 == 0 else nc.sync
            eng.dma_start(out=out_2[0][4 * q : 4 * q + 4, :].bitcast(I32), in_=y_sc[32 * q : 32 * q + 4, :].bitcast(I32))
